import numpy as np
import ml_dtypes


def mxq(x, axis, fmt="e4m3"):
    dtype, down = {"e4m3": (ml_dtypes.float8_e4m3fn, 7), "e5m2": (ml_dtypes.float8_e5m2, 14)}[fmt]
    v = np.moveaxis(np.asarray(x, np.float32).astype(ml_dtypes.bfloat16).astype(np.float64), axis, -1)
    blocks = v.reshape(v.shape[:-1] + (-1, 32))
    amax = np.abs(blocks).max(-1, keepdims=True)
    byte = np.maximum(np.where(amax > 0, np.frexp(amax)[1] - 1 + 127, 0) - down, 1)
    scale = np.exp2(byte - 127.0)
    codes = (blocks / scale).astype(np.float32).astype(dtype).astype(np.float64)
    return np.moveaxis((codes * scale).reshape(v.shape), -1, axis)


WIDE = False


def mx_kscale(k):
    if not WIDE:
        return np.ones(k)
    levels = np.array([10, -10, 5, -5, 0])
    if k % 512:
        return np.exp2(np.random.permutation(np.resize(levels, k // 32))).repeat(32)
    a = np.empty((k // 512, 16))
    for p in range(k // 512):
        a[p, :8] = np.random.permutation(np.resize(levels, 8))
        for g in range(8):
            far = levels[np.abs(levels - a[p, g]) >= 10]
            a[p, g + 8] = far[np.random.randint(len(far))]
    return np.exp2(a.ravel()).repeat(32)


def f64(x):
    return np.asarray(x).astype(np.float64)


def striped(idx):
    return np.tile(idx.reshape(-1, 16).T, (8, 1)).astype(np.uint16)


def unstriped(offs):
    return offs[:16].T.reshape(-1).astype(np.int64)


E2M1 = np.array([0.0, 0.5, 1.0, 1.5, 2.0, 3.0, 4.0, 6.0, -0.0, -0.5, -1.0, -1.5, -2.0, -3.0, -4.0, -6.0])


def pack_weight(w, fmt):
    k, n = w.shape
    w = f64(np.asarray(w, np.float32).astype(ml_dtypes.bfloat16)).reshape(k // 32, 32, n)
    amax = np.abs(w).max(1)
    if fmt == "e4m3":
        byte = np.frexp(amax)[1] - 1 + 127 - 7
    else:
        mant, ex = np.frexp(amax / 6.0)
        byte = np.where(mant > 0.5, ex, ex - 1) + 127
    byte = np.clip(np.where(amax > 0, byte, 1), 1, 254)
    scaled = (w * np.exp2(127.0 - byte)[:, None, :]).reshape(k, n).astype(np.float32)
    by_word = np.ascontiguousarray(scaled.reshape(k // 512, 128, 4, n).transpose(0, 1, 3, 2))
    if fmt == "e4m3":
        words = by_word.astype(ml_dtypes.float8_e4m3fn).view(np.uint8)
    else:
        c = by_word.astype(ml_dtypes.float4_e2m1fn).view(np.uint8) & 0xF
        words = (c[..., 0::2] | (c[..., 1::2] << 4)).reshape(k // 512, 128, 2 * n)
    return np.ascontiguousarray(words), np.ascontiguousarray(byte.astype(np.uint8).reshape(k // 512, 16, n))


def unpack_weight(words, scales, fmt):
    g, _, n = scales.shape
    words = np.ascontiguousarray(words).reshape(g, 128, n, -1)
    if fmt == "e4m3":
        vals = words.view(ml_dtypes.float8_e4m3fn).astype(np.float64)
    else:
        nib = np.empty((g, 128, n, 4), np.uint8)
        nib[..., 0::2] = words & 0xF
        nib[..., 1::2] = words >> 4
        vals = E2M1[nib]
    vals = vals * np.repeat(np.exp2(scales.astype(np.float64) - 127.0), 8, axis=1)[..., None]
    return vals.transpose(0, 1, 3, 2).reshape(g * 512, n)


def gelu(v):
    return 0.5 * v * (1.0 + np.tanh(np.sqrt(2.0 / np.pi) * (v + 0.044715 * v**3)))


def bf(x):
    return np.asarray(x, np.float32).astype(ml_dtypes.bfloat16)


def planes(Y):
    n, m = Y.shape
    b = f64(bf(Y)).reshape(n // 32, 32, m)
    amax = np.abs(b).max(1)
    byte = np.clip(np.where(amax > 0, np.frexp(amax)[1] - 1 + 127 - 7, 1), 1, 254)
    codes = (b * np.exp2(127.0 - byte)[:, None, :]).reshape(n, m).astype(np.float32).astype(ml_dtypes.float8_e4m3fn).view(np.uint8)
    words = codes.reshape(n // 512, 128, 4, m).transpose(0, 1, 3, 2)
    return np.ascontiguousarray(words), np.ascontiguousarray(byte.astype(np.uint8).reshape(n // 512, 16, m))


K, T, S, P, H, N = 1024, 4096, 1024, 512, 512, 1024

def setup_inputs():
    n = np.random.standard_normal
    s = mx_kscale(K)[:, None]
    u = mx_kscale(H)[:, None]
    d = {}
    d["tab_words"], d["tab_scales"] = pack_weight(n((K, T)) * s, "e4m3")
    d["offs"] = striped(np.random.permutation(T)[:S])
    d["pos1"] = striped(np.random.permutation(S)[:P])
    d["pos2"] = striped(np.random.permutation(S)[:P])
    d["w1"] = (n((K, H)) / K ** 0.5 / s).astype(np.float32)
    d["w2_words"], d["w2_scales"] = pack_weight(n((K, H)) / K ** 0.5 / s, "e2m1")
    d["gain"] = (np.exp(0.3 * n(H)) * u[:, 0]).astype(np.float32)
    d["w3"] = (0.8 * n((H, N)) / H ** 0.5 / u).astype(np.float32)
    d["going"] = n((N, S)).astype(np.float32)
    d["sheet"] = (n((N, P)) * np.exp(0.8 * n(N))[:, None]).astype(np.float32)
    return d

def reference(tab_words, tab_scales, offs, pos1, pos2, w1, w2_words, w2_scales, gain, w3, going, sheet):
    v = unpack_weight(tab_words, tab_scales, "e4m3")[:, unstriped(offs)]
    w2 = unpack_weight(w2_words, w2_scales, "e2m1")
    a = mxq(f64(w1), 0, "e4m3").T @ v
    b = w2.T @ v
    h = f64(gain)[:, None] * (a * np.square(b))
    g2 = (mxq(f64(w3), 0, "e4m3").T @ mxq(h, 0, "e4m3")) + f64(going)
    diff = g2[:, unstriped(pos1)] - g2[:, unstriped(pos2)]
    y = f64(sheet) * (1.0 / (1.0 + np.exp(-diff)))
    words, scales = planes(y)
    return y, words, scales

@@ -1,0 +1,229 @@
+from contextlib import ExitStack
+
+import concourse.mybir as mybir
+
+K, T, S, M, H, N = 1024, 4096, 1024, 512, 512, 1024
+FLOPS = 2 * K * H * S * 2 + 2 * H * N * S
+
+F32 = mybir.dt.float32
+BF16 = mybir.dt.bfloat16
+I32 = mybir.dt.int32
+U32 = mybir.dt.uint32
+U16 = mybir.dt.uint16
+U8 = mybir.dt.uint8
+FP8X4 = mybir.dt.float8_e4m3fn_x4
+FP4X4 = mybir.dt.float4_e2m1fn_x4
+ALU = mybir.AluOpType
+ACT = mybir.ActivationFunctionType
+P = 128
+BANK = 512
+
+
+def tile_list_rival_form_scores_kernel(tc, tab_words, tab_scales, offs, pos1, pos2, w1, w2_words, w2_scales,
+                                                 gain, w3, going, sheet, out_0, out_1, out_2):
+    nc = tc.nc
+    with ExitStack() as ctx:
+        held = ctx.enter_context(tc.tile_pool(name="held", bufs=1))
+        ring = ctx.enter_context(tc.tile_pool(name="ring", bufs=2))
+        psum = ctx.enter_context(tc.psum_pool(name="psum", bufs=8))
+
+        def copy_on(engine, out, in_):
+            if engine == "scalar":
+                nc.scalar.copy(out=out, in_=in_)
+            else:
+                nc.vector.tensor_copy(out=out, in_=in_)
+
+        def staged():
+            return ring.tile([P, 1024], BF16, name="staged", tag="staged", bufs=8, align_bytes=64)
+
+        tab_sc = held.tile([P, 2 * T], U8, name="tab_sc", align_bytes=64)
+        w2_sc_raw = held.tile([P, 2 * H], U8, name="w2_sc_raw", align_bytes=64)
+        nc.vector.memset(tab_sc[:].bitcast(I32), 0)
+        nc.vector.memset(w2_sc_raw[:].bitcast(I32), 0)
+        for q in range(4):
+            nc.sync.dma_start(out=tab_sc[32 * q:32 * q + 4, :].bitcast(I32).rearrange("r (a t) -> r a t", a=2),
+                                in_=tab_scales[:, 4 * q:4 * q + 4, :].rearrange("a r t -> r a t").bitcast(I32))
+        for q in range(4):
+            nc.sync.dma_start(out=w2_sc_raw[32 * q:32 * q + 4, :].bitcast(I32).rearrange("r (a c) -> r a c", a=2),
+                                in_=w2_scales[:, 4 * q:4 * q + 4, :].rearrange("a r c -> r a c").bitcast(I32))
+
+        offs_sb = held.tile([P, S // 16], U16, name="offs_sb")
+        nc.sync.dma_start(offs_sb[:], offs)
+        pos1_sb = held.tile([P, M // 16], U16, name="pos1_sb")
+        nc.sync.dma_start(pos1_sb[:], pos1)
+        pos2_sb = held.tile([P, M // 16], U16, name="pos2_sb")
+        nc.sync.dma_start(pos2_sb[:], pos2)
+        gain_sb = held.tile([P, 4], F32, name="gain_sb")
+        nc.sync.dma_start(out=gain_sb[:], in_=gain.rearrange("(p t) -> p t", t=4))
+        w2_raw = held.tile([P, 4 * H], U8, name="w2_raw", align_bytes=64)
+        nc.sync.dma_start(out=w2_raw[:].bitcast(I32).rearrange("p (a c) -> p a c", a=2),
+                          in_=w2_words.rearrange("a p c -> p a c").bitcast(I32))
+        w1_raw = [held.tile([P, 4, H], F32, name="w1_raw%d" % a) for a in range(2)]
+        tab_w = [held.tile([P, T], I32, name="tab_w%d" % a, align_bytes=64) for a in range(2)]
+        w1_rows = w1.rearrange("(a p i) r -> a p i r", a=2, i=4)
+        nc.sync.dma_start(out=w1_raw[0][:], in_=w1_rows[0])
+        for a in range(2):
+            nc.sync.dma_start(out=tab_w[a][:], in_=tab_words[a].rearrange("p t i -> p (t i)").bitcast(I32))
+        nc.sync.dma_start(out=w1_raw[1][:], in_=w1_rows[1])
+        w3_raw = [held.tile([P, 4, BANK], F32, name="w3_raw%d" % g) for g in range(2)]
+        w3_rows = w3.rearrange("(p i) (g n) -> g p i n", i=4, g=2)
+        nc.sync.dma_start(out=w3_raw[0][:], in_=w3_rows[0])
+
+        going_rows = going.rearrange("(g p t) j -> g t p j", g=2, t=4)
+        sheet_rows = sheet.rearrange("(g p t) m -> g p t m", g=2, t=4)
+        out_rows = out_0.rearrange("(g p t) m -> g t p m", g=2, t=4)
+        first_slot = held.tile([P, S], F32, name="first_slot")
+        slots = [held.tile([P, 4, S], F32, name="slots%d" % g) for g in range(2)]
+        sheet_sb = [held.tile([P, 4, M], F32, name="sheet_sb%d" % g) for g in range(2)]
+
+        def slot(i):
+            return first_slot[:] if i == 0 else slots[(i - 1) // 4][:, (i - 1) % 4, :]
+
+        def load_going(i):
+            nc.sync.dma_start(out=slot(i), in_=going_rows[i // 4, i % 4])
+
+        load_going(0)
+        load_going(1)
+        nc.sync.dma_start(out=sheet_sb[0][:], in_=sheet_rows[0])
+        load_going(2)
+        load_going(3)
+        nc.sync.dma_start(out=w3_raw[1][:], in_=w3_rows[1])
+        for i in range(4, 8):
+            load_going(i)
+        nc.sync.dma_start(out=sheet_sb[1][:], in_=sheet_rows[1])
+
+        w2_codes = held.tile([P, 4 * H], U8, name="w2_codes", align_bytes=64)
+        w2_sc = held.tile([P, 2 * H], U8, name="w2_sc", align_bytes=64)
+        nc.vector.tensor_copy(out=w2_codes[:].bitcast(U16).rearrange("p (a t m) -> p a m t", a=2, t=4),
+                              in_=w2_raw[:].bitcast(U16).rearrange("p (a m t) -> p a m t", a=2, t=4))
+
+        def quantize_weight(raw, codes, scales, engines):
+            for u in range(2):
+                grouped = staged()
+                copy_on(engines[u], grouped[:].rearrange("p (t m i) -> p m i t", t=2, i=4),
+                        raw[:].rearrange("p i (m t) -> p m i t", t=4)[:, :, :, 2 * u:2 * u + 2])
+                cols = slice(256 * u, 256 * (u + 1))
+                nc.vector.quantize_mx(out=codes[:, cols].bitcast(FP8X4), scales=scales[:, cols], in_=grouped[:])
+
+        w1_codes = [held.tile([P, H], U32, name="w1_codes%d" % a, align_bytes=64) for a in range(2)]
+        w1_sc = [held.tile([P, H], U8, name="w1_sc%d" % a, align_bytes=64) for a in range(2)]
+        w3_codes = [held.tile([P, BANK], U32, name="w3_codes%d" % g, align_bytes=64) for g in range(2)]
+        w3_sc = [held.tile([P, BANK], U8, name="w3_sc%d" % g, align_bytes=64) for g in range(2)]
+        quantize_weight(w1_raw[0], w1_codes[0], w1_sc[0], ("scalar", "scalar"))
+
+        v_codes = [[held.tile([P, BANK], U32, name="v_codes%d%d" % (a, c), align_bytes=64) for c in range(2)] for a in range(2)]
+        v_sc = [held.tile([P, S], U8, name="v_sc%d" % a, align_bytes=64) for a in range(2)]
+        for a in range(2):
+            nc.vector.tensor_copy(v_sc[a][:], tab_sc[:, a * T:(a + 1) * T].indirect(offs_sb[:]))
+            if a == 0:
+                nc.vector.tensor_copy(out=w2_sc[:].rearrange("p (a t m) -> p a m t", a=2, t=4),
+                                      in_=w2_sc_raw[:].rearrange("p (a m t) -> p a m t", a=2, t=4))
+            for c in range(2):
+                nc.vector.tensor_copy(v_codes[a][c][:], tab_w[a][:].bitcast(U32).indirect(offs_sb[:, 32 * c:32 * (c + 1)]))
+        quantize_weight(w1_raw[1], w1_codes[1], w1_sc[1], ("vector", "scalar"))
+
+        squares = {}
+        for c in range(2):
+            for t in range(4):
+                b_bank = psum.tile([P, BANK], F32, name="b_bank", tag="bank")
+                for a in range(2):
+                    col = 4 * a + t
+                    nc.tensor.matmul_mx(out=b_bank[:], lhsT=w2_codes[:, 256 * col:256 * (col + 1)].bitcast(FP4X4),
+                                        lhsT_scale=w2_sc[:, P * col:P * (col + 1)],
+                                        rhs=v_codes[a][c][:].bitcast(FP8X4), rhs_scale=v_sc[a][:, BANK * c:BANK * (c + 1)],
+                                        start=(a == 0), stop=(a == 1))
+                square = ring.tile([P, BANK], F32, name="square", tag="square", bufs=8)
+                nc.scalar.activation(out=square[:], in_=b_bank[:], func=ACT.Square)
+                squares[c, t] = square
+        quantize_weight(w3_raw[0], w3_codes[0], w3_sc[0], ("scalar", "scalar"))
+        h_codes = held.tile([P, S], U32, name="h_codes", align_bytes=64)
+        h_sc = held.tile([P, S], U8, name="h_sc", align_bytes=64)
+        h_rows = [held.tile([P, 4, BANK], BF16, name="h_rows%d" % c) for c in range(2)]
+        for c in range(2):
+            for t in range(4):
+                a_bank = psum.tile([P, BANK], F32, name="a_bank", tag="bank")
+                for a in range(2):
+                    nc.tensor.matmul_mx(out=a_bank[:], lhsT=w1_codes[a][:, P * t:P * (t + 1)].bitcast(FP8X4),
+                                        lhsT_scale=w1_sc[a][:, P * t:P * (t + 1)],
+                                        rhs=v_codes[a][c][:].bitcast(FP8X4), rhs_scale=v_sc[a][:, BANK * c:BANK * (c + 1)],
+                                        start=(a == 0), stop=(a == 1))
+                nc.vector.scalar_tensor_tensor(out=h_rows[c][:, t, :], in0=a_bank[:], scalar=gain_sb[:, t:t + 1],
+                                               in1=squares[c, t][:], op0=ALU.mult, op1=ALU.mult)
+
+        def interleave(engine, rows):
+            grouped = staged()
+            copy_on(engine, grouped[:].rearrange("p (c i t) -> p c t i", i=4, t=4),
+                    rows.rearrange("p t (c i) -> p c t i", i=4))
+            return grouped
+
+        h_grouped = [interleave(("scalar", "vector")[piece // 2], h_rows[piece // 2][:, :, 256 * (piece % 2):256 * (piece % 2 + 1)])
+                     for piece in range(4)]
+        for piece in range(4):
+            cols = slice(256 * piece, 256 * (piece + 1))
+            nc.vector.quantize_mx(out=h_codes[:, cols].bitcast(FP8X4), scales=h_sc[:, cols], in_=h_grouped[piece][:])
+
+        y_codes = [held.tile([P, M], U32, name="y_codes%d" % g, align_bytes=64) for g in range(2)]
+        y_sc = [held.tile([P, M], U8, name="y_sc%d" % g, align_bytes=64) for g in range(2)]
+        scores = {}
+
+        def score(i, c):
+            g, t = divmod(i, 4)
+            if c == 0:
+                scores[i] = ring.tile([P, S], F32, name="scores", tag="scores", bufs=3)
+            cols = slice(BANK * c, BANK * (c + 1))
+            bank = psum.tile([P, BANK], F32, name="score_bank", tag="bank")
+            nc.tensor.matmul_mx(out=bank[:], lhsT=w3_codes[g][:, P * t:P * (t + 1)].bitcast(FP8X4),
+                                lhsT_scale=w3_sc[g][:, P * t:P * (t + 1)],
+                                rhs=h_codes[:, cols].bitcast(FP8X4), rhs_scale=h_sc[:, cols], start=True, stop=True)
+            nc.vector.tensor_tensor(out=scores[i][:, cols], in0=bank[:], in1=slot(i)[:, cols], op=ALU.add)
+
+        def pick_second(i, m0, m1):
+            second = ring.tile([P, M], F32, name="second", tag="second", bufs=2)
+            nc.vector.tensor_copy(second[:, :m1 - m0], scores[i][:].indirect(pos2_sb[:, m0 // 16:m1 // 16]))
+            return second
+
+        def compare(i, m0, m1, second):
+            diff = slot(i + 1)[:, m0:m1]
+            nc.vector.tensor_tensor(diff, scores[i][:].indirect(pos1_sb[:, m0 // 16:m1 // 16]), second[:, :m1 - m0], ALU.subtract)
+            odds = ring.tile([P, M], F32, name="odds", tag="odds", bufs=2)
+            nc.scalar.activation(out=odds[:, :m1 - m0], in_=diff, func=ACT.Sigmoid)
+            return odds
+
+        def weigh(i, m0, m1, odds):
+            g, t = divmod(i, 4)
+            y = slot(i + 1)[:, M + m0:M + m1]
+            nc.vector.tensor_tensor(out=y, in0=odds[:, :m1 - m0], in1=sheet_sb[g][:, t, m0:m1], op=ALU.mult)
+            nc.sync.dma_start(out=out_rows[g, t][:, m0:m1], in_=y)
+
+        def planes(g, half, engine):
+            m0, m1 = 256 * half, 256 * (half + 1)
+            grouped = interleave(engine, slots[g][:, :, M + m0:M + m1])
+            nc.vector.quantize_mx(out=y_codes[g][:, m0:m1].bitcast(FP8X4), scales=y_sc[g][:, m0:m1], in_=grouped[:])
+            nc.sync.dma_start(out=out_1[g].rearrange("p m t -> p (m t)").bitcast(I32)[:, m0:m1],
+                              in_=y_codes[g][:, m0:m1].bitcast(I32))
+
+        def store_scales(g):
+            for q in range(4):
+                nc.sync.dma_start(out=out_2[g, 4 * q:4 * q + 4, :].bitcast(I32), in_=y_sc[g][32 * q:32 * q + 4, :].bitcast(I32))
+
+        score(0, 0)
+        score(0, 1)
+        for i in range(7):
+            second = pick_second(i, 0, M)
+            score(i + 1, 0)
+            score(i + 1, 1)
+            odds = compare(i, 0, M, second)
+            weigh(i, 0, M, odds)
+            if i == 1:
+                quantize_weight(w3_raw[1], w3_codes[1], w3_sc[1], ("scalar", "scalar"))
+            if i == 3:
+                planes(0, 0, "scalar")
+                planes(0, 1, "scalar")
+                store_scales(0)
+        seconds = [pick_second(7, 256 * half, 256 * (half + 1)) for half in range(2)]
+        odds_halves = [compare(7, 256 * half, 256 * (half + 1), seconds[half]) for half in range(2)]
+        for half in range(2):
+            weigh(7, 256 * half, 256 * (half + 1), odds_halves[half])
+        planes(1, 0, "scalar")
+        planes(1, 1, "vector")
+        store_scales(1)

@@ -1,6 +1,7 @@
 from contextlib import ExitStack
 
 import concourse.mybir as mybir
+from concourse.masks import make_identity
 
 K, T, S, M, H, N = 1024, 4096, 1024, 512, 512, 1024
 FLOPS = 2 * K * H * S * 2 + 2 * H * N * S
@@ -25,7 +26,7 @@ def tile_list_rival_form_scores_kernel(tc, tab_words, tab_scales, offs, pos1, po
     with ExitStack() as ctx:
         held = ctx.enter_context(tc.tile_pool(name="held", bufs=1))
         ring = ctx.enter_context(tc.tile_pool(name="ring", bufs=2))
-        psum = ctx.enter_context(tc.psum_pool(name="psum", bufs=8))
+        psum = ctx.enter_context(tc.psum_pool(name="psum", bufs=2))
 
         def copy_on(engine, out, in_):
             if engine == "scalar":
@@ -43,9 +44,15 @@ def tile_list_rival_form_scores_kernel(tc, tab_words, tab_scales, offs, pos1, po
         for q in range(4):
             nc.sync.dma_start(out=tab_sc[32 * q:32 * q + 4, :].bitcast(I32).rearrange("r (a t) -> r a t", a=2),
                                 in_=tab_scales[:, 4 * q:4 * q + 4, :].rearrange("a r t -> r a t").bitcast(I32))
-        for q in range(4):
-            nc.sync.dma_start(out=w2_sc_raw[32 * q:32 * q + 4, :].bitcast(I32).rearrange("r (a c) -> r a c", a=2),
-                                in_=w2_scales[:, 4 * q:4 * q + 4, :].rearrange("a r c -> r a c").bitcast(I32))
+
+        def four_rows():
+            return ring.tile([P, 4, BANK], F32, name="four_rows", tag="four_rows", bufs=5)
+
+        tab_w = [held.tile([P, T], I32, name="tab_w%d" % a, align_bytes=64) for a in range(2)]
+        tab_rows = [tab_words[a].rearrange("p t i -> p (t i)").bitcast(I32) for a in range(2)]
+
+        def load_table_columns(a, first, last):
+            nc.sync.dma_start(out=tab_w[a][:, first:last], in_=tab_rows[a][:, first:last])
 
         offs_sb = held.tile([P, S // 16], U16, name="offs_sb")
         nc.sync.dma_start(offs_sb[:], offs)
@@ -56,60 +63,69 @@ def tile_list_rival_form_scores_kernel(tc, tab_words, tab_scales, offs, pos1, po
         gain_sb = held.tile([P, 4], F32, name="gain_sb")
         nc.sync.dma_start(out=gain_sb[:], in_=gain.rearrange("(p t) -> p t", t=4))
         w2_raw = held.tile([P, 4 * H], U8, name="w2_raw", align_bytes=64)
-        nc.sync.dma_start(out=w2_raw[:].bitcast(I32).rearrange("p (a c) -> p a c", a=2),
-                          in_=w2_words.rearrange("a p c -> p a c").bitcast(I32))
-        w1_raw = [held.tile([P, 4, H], F32, name="w1_raw%d" % a) for a in range(2)]
-        tab_w = [held.tile([P, T], I32, name="tab_w%d" % a, align_bytes=64) for a in range(2)]
-        w1_rows = w1.rearrange("(a p i) r -> a p i r", a=2, i=4)
-        nc.sync.dma_start(out=w1_raw[0][:], in_=w1_rows[0])
         for a in range(2):
-            nc.sync.dma_start(out=tab_w[a][:], in_=tab_words[a].rearrange("p t i -> p (t i)").bitcast(I32))
-        nc.sync.dma_start(out=w1_raw[1][:], in_=w1_rows[1])
-        w3_raw = [held.tile([P, 4, BANK], F32, name="w3_raw%d" % g) for g in range(2)]
+            nc.sync.dma_start(out=w2_raw[:, 2 * H * a:2 * H * (a + 1)].bitcast(I32), in_=w2_words[a].bitcast(I32))
+        load_table_columns(0, 0, 1536)
+        load_table_columns(0, 1536, 3072)
+        load_table_columns(0, 3072, T)
+        load_table_columns(1, 0, 3072)
+        for q in range(4):
+            nc.sync.dma_start(out=w2_sc_raw[32 * q:32 * q + 4, :].bitcast(I32).rearrange("r (a c) -> r a c", a=2),
+                                in_=w2_scales[:, 4 * q:4 * q + 4, :].rearrange("a r c -> r a c").bitcast(I32))
+        load_table_columns(1, 3072, T)
+        w1_raw = [four_rows() for a in range(2)]
+        w1_rows = w1.rearrange("(a p i) r -> a p i r", a=2, i=4)
+        for a in range(2):
+            nc.sync.dma_start(out=w1_raw[a][:], in_=w1_rows[a])
+        w3_raw = [four_rows() for g in range(2)]
         w3_rows = w3.rearrange("(p i) (g n) -> g p i n", i=4, g=2)
         nc.sync.dma_start(out=w3_raw[0][:], in_=w3_rows[0])
 
         going_rows = going.rearrange("(g p t) j -> g t p j", g=2, t=4)
         sheet_rows = sheet.rearrange("(g p t) m -> g p t m", g=2, t=4)
         out_rows = out_0.rearrange("(g p t) m -> g t p m", g=2, t=4)
-        first_slot = held.tile([P, S], F32, name="first_slot")
-        slots = [held.tile([P, 4, S], F32, name="slots%d" % g) for g in range(2)]
-        sheet_sb = [held.tile([P, 4, M], F32, name="sheet_sb%d" % g) for g in range(2)]
-
-        def slot(i):
-            return first_slot[:] if i == 0 else slots[(i - 1) // 4][:, (i - 1) % 4, :]
+        sheet_sb = {}
+        pages = {}
 
         def load_going(i):
-            nc.sync.dma_start(out=slot(i), in_=going_rows[i // 4, i % 4])
+            pages[i] = ring.tile([P, 2 * S], F32, name="page", tag="page", bufs=8)
+            nc.sync.dma_start(out=pages[i][:, S:], in_=going_rows[i // 4, i % 4])
+
+        def load_sheet(g):
+            sheet_sb[g] = four_rows()
+            nc.sync.dma_start(out=sheet_sb[g][:], in_=sheet_rows[g])
 
         load_going(0)
         load_going(1)
-        nc.sync.dma_start(out=sheet_sb[0][:], in_=sheet_rows[0])
-        load_going(2)
-        load_going(3)
         nc.sync.dma_start(out=w3_raw[1][:], in_=w3_rows[1])
+        load_going(2)
+        load_sheet(0)
+        load_going(3)
         for i in range(4, 8):
             load_going(i)
-        nc.sync.dma_start(out=sheet_sb[1][:], in_=sheet_rows[1])
+        identity = held.tile([P, P], F32, name="identity")
+        make_identity(nc, identity[:])
 
         w2_codes = held.tile([P, 4 * H], U8, name="w2_codes", align_bytes=64)
         w2_sc = held.tile([P, 2 * H], U8, name="w2_sc", align_bytes=64)
         nc.vector.tensor_copy(out=w2_codes[:].bitcast(U16).rearrange("p (a t m) -> p a m t", a=2, t=4),
                               in_=w2_raw[:].bitcast(U16).rearrange("p (a m t) -> p a m t", a=2, t=4))
 
+        def quantize_weight_half(raw, codes, scales, u, engine):
+            grouped = staged()
+            copy_on(engine, grouped[:].rearrange("p (t m i) -> p m i t", t=2, i=4),
+                    raw[:].rearrange("p i (m t) -> p m i t", t=4)[:, :, :, 2 * u:2 * u + 2])
+            cols = slice(256 * u, 256 * (u + 1))
+            nc.vector.quantize_mx(out=codes[:, cols].bitcast(FP8X4), scales=scales[:, cols], in_=grouped[:])
+
         def quantize_weight(raw, codes, scales, engines):
             for u in range(2):
-                grouped = staged()
-                copy_on(engines[u], grouped[:].rearrange("p (t m i) -> p m i t", t=2, i=4),
-                        raw[:].rearrange("p i (m t) -> p m i t", t=4)[:, :, :, 2 * u:2 * u + 2])
-                cols = slice(256 * u, 256 * (u + 1))
-                nc.vector.quantize_mx(out=codes[:, cols].bitcast(FP8X4), scales=scales[:, cols], in_=grouped[:])
+                quantize_weight_half(raw, codes, scales, u, engines[u])
 
         w1_codes = [held.tile([P, H], U32, name="w1_codes%d" % a, align_bytes=64) for a in range(2)]
         w1_sc = [held.tile([P, H], U8, name="w1_sc%d" % a, align_bytes=64) for a in range(2)]
         w3_codes = [held.tile([P, BANK], U32, name="w3_codes%d" % g, align_bytes=64) for g in range(2)]
         w3_sc = [held.tile([P, BANK], U8, name="w3_sc%d" % g, align_bytes=64) for g in range(2)]
-        quantize_weight(w1_raw[0], w1_codes[0], w1_sc[0], ("scalar", "scalar"))
 
         v_codes = [[held.tile([P, BANK], U32, name="v_codes%d%d" % (a, c), align_bytes=64) for c in range(2)] for a in range(2)]
         v_sc = [held.tile([P, S], U8, name="v_sc%d" % a, align_bytes=64) for a in range(2)]
@@ -120,12 +136,13 @@ def tile_list_rival_form_scores_kernel(tc, tab_words, tab_scales, offs, pos1, po
                                       in_=w2_sc_raw[:].rearrange("p (a m t) -> p a m t", a=2, t=4))
             for c in range(2):
                 nc.vector.tensor_copy(v_codes[a][c][:], tab_w[a][:].bitcast(U32).indirect(offs_sb[:, 32 * c:32 * (c + 1)]))
+        quantize_weight(w1_raw[0], w1_codes[0], w1_sc[0], ("scalar", "vector"))
         quantize_weight(w1_raw[1], w1_codes[1], w1_sc[1], ("vector", "scalar"))
 
         squares = {}
         for c in range(2):
             for t in range(4):
-                b_bank = psum.tile([P, BANK], F32, name="b_bank", tag="bank")
+                b_bank = psum.tile([P, BANK], F32, name="b_bank", tag="product", bufs=4)
                 for a in range(2):
                     col = 4 * a + t
                     nc.tensor.matmul_mx(out=b_bank[:], lhsT=w2_codes[:, 256 * col:256 * (col + 1)].bitcast(FP4X4),
@@ -141,7 +158,7 @@ def tile_list_rival_form_scores_kernel(tc, tab_words, tab_scales, offs, pos1, po
         h_rows = [held.tile([P, 4, BANK], BF16, name="h_rows%d" % c) for c in range(2)]
         for c in range(2):
             for t in range(4):
-                a_bank = psum.tile([P, BANK], F32, name="a_bank", tag="bank")
+                a_bank = psum.tile([P, BANK], F32, name="a_bank", tag=("diff", "odds")[t % 2])
                 for a in range(2):
                     nc.tensor.matmul_mx(out=a_bank[:], lhsT=w1_codes[a][:, P * t:P * (t + 1)].bitcast(FP8X4),
                                         lhsT_scale=w1_sc[a][:, P * t:P * (t + 1)],
@@ -164,66 +181,96 @@ def tile_list_rival_form_scores_kernel(tc, tab_words, tab_scales, offs, pos1, po
 
         y_codes = [held.tile([P, M], U32, name="y_codes%d" % g, align_bytes=64) for g in range(2)]
         y_sc = [held.tile([P, M], U8, name="y_sc%d" % g, align_bytes=64) for g in range(2)]
-        scores = {}
+        load_sheet(1)
+        y_rows = [four_rows() for g in range(2)]
+        first_pick = held.tile([P, M], F32, name="first_pick")
+        odds_banks = {}
 
-        def score(i, c):
+        def score(i):
             g, t = divmod(i, 4)
-            if c == 0:
-                scores[i] = ring.tile([P, S], F32, name="scores", tag="scores", bufs=3)
-            cols = slice(BANK * c, BANK * (c + 1))
-            bank = psum.tile([P, BANK], F32, name="score_bank", tag="bank")
-            nc.tensor.matmul_mx(out=bank[:], lhsT=w3_codes[g][:, P * t:P * (t + 1)].bitcast(FP8X4),
-                                lhsT_scale=w3_sc[g][:, P * t:P * (t + 1)],
-                                rhs=h_codes[:, cols].bitcast(FP8X4), rhs_scale=h_sc[:, cols], start=True, stop=True)
-            nc.vector.tensor_tensor(out=scores[i][:, cols], in0=bank[:], in1=slot(i)[:, cols], op=ALU.add)
+            page = pages[i]
+            for c in range(2):
+                cols = slice(BANK * c, BANK * (c + 1))
+                given = page[:, S + BANK * c:S + BANK * (c + 1)]
+                bank = psum.tile([P, BANK], F32, name="score_bank", tag="product", bufs=4)
+                nc.tensor.matmul_mx(out=bank[:], lhsT=w3_codes[g][:, P * t:P * (t + 1)].bitcast(FP8X4),
+                                    lhsT_scale=w3_sc[g][:, P * t:P * (t + 1)],
+                                    rhs=h_codes[:, cols].bitcast(FP8X4), rhs_scale=h_sc[:, cols], start=True, stop=True)
+                if i == 0:
+                    nc.vector.tensor_tensor(out=page[:, cols], in0=bank[:], in1=given, op=ALU.add)
+                else:
+                    nc.scalar.copy(out=page[:, cols], in_=bank[:])
+            if i > 0:
+                nc.gpsimd.tensor_tensor(out=page[:, :S], in0=page[:, :S], in1=page[:, S:], op=ALU.add)
 
-        def pick_second(i, m0, m1):
-            second = ring.tile([P, M], F32, name="second", tag="second", bufs=2)
-            nc.vector.tensor_copy(second[:, :m1 - m0], scores[i][:].indirect(pos2_sb[:, m0 // 16:m1 // 16]))
-            return second
+        def y_of(i):
+            return y_rows[i // 4][:, i % 4, :]
 
-        def compare(i, m0, m1, second):
-            diff = slot(i + 1)[:, m0:m1]
-            nc.vector.tensor_tensor(diff, scores[i][:].indirect(pos1_sb[:, m0 // 16:m1 // 16]), second[:, :m1 - m0], ALU.subtract)
-            odds = ring.tile([P, M], F32, name="odds", tag="odds", bufs=2)
-            nc.scalar.activation(out=odds[:, :m1 - m0], in_=diff, func=ACT.Sigmoid)
-            return odds
+        def compare(i):
+            plus = first_pick[:] if i == 0 else y_of(i - 1)
+            nc.vector.tensor_copy(plus, pages[i][:].indirect(pos1_sb[:]))
+            minus = ring.tile([P, M], F32, name="minus", tag="minus", bufs=2)
+            nc.vector.tensor_scalar(minus[:], pages[i][:].indirect(pos2_sb[:]), -1.0, 0.0, ALU.mult, ALU.add)
+            diff_bank = psum.tile([P, BANK], F32, name="diff_bank", tag="diff")
+            for term, picked in enumerate((plus, minus[:])):
+                for b in range(4):
+                    nc.tensor.matmul(diff_bank[:, P * b:P * (b + 1)], lhsT=picked[:, P * b:P * (b + 1)], rhs=identity[:],
+                                     is_transpose=True, start=(term == 0 and b == 0), stop=(term == 1 and b == 3))
+            odds_turned = ring.tile([P, M], F32, name="odds_turned", tag="odds_turned", bufs=2)
+            nc.scalar.activation(out=odds_turned[:], in_=diff_bank[:], func=ACT.Sigmoid)
+            odds_banks[i] = psum.tile([P, BANK], F32, name="odds_bank", tag="odds")
+            for b in range(4):
+                nc.tensor.transpose(odds_banks[i][:, P * b:P * (b + 1)], odds_turned[:, P * b:P * (b + 1)], identity[:])
 
-        def weigh(i, m0, m1, odds):
+        def weigh(i):
             g, t = divmod(i, 4)
-            y = slot(i + 1)[:, M + m0:M + m1]
-            nc.vector.tensor_tensor(out=y, in0=odds[:, :m1 - m0], in1=sheet_sb[g][:, t, m0:m1], op=ALU.mult)
-            nc.sync.dma_start(out=out_rows[g, t][:, m0:m1], in_=y)
+            nc.vector.tensor_tensor(out=y_of(i), in0=odds_banks[i][:], in1=sheet_sb[g][:, t, :], op=ALU.mult)
+            nc.sync.dma_start(out=out_rows[g, t], in_=y_of(i))
+
+        def finish_last_tile():
+            page = pages[7]
+            halves = [slice(256 * half, 256 * (half + 1)) for half in range(2)]
+            entries = [slice(16 * half, 16 * (half + 1)) for half in range(2)]
+            minus = [y_of(6)[:, halves[0]], first_pick[:, halves[1]]]
+            diff = ring.tile([P, M], F32, name="minus", tag="minus", bufs=2)
+            odds = ring.tile([P, M], F32, name="odds_turned", tag="odds_turned", bufs=2)
+            for half in range(2):
+                nc.vector.tensor_copy(minus[half], page[:].indirect(pos2_sb[:, entries[half]]))
+            for half in range(2):
+                nc.vector.tensor_tensor(diff[:, halves[half]], page[:].indirect(pos1_sb[:, entries[half]]), minus[half], ALU.subtract)
+                nc.scalar.activation(out=odds[:, halves[half]], in_=diff[:, halves[half]], func=ACT.Sigmoid)
+                if half == 0:
+                    weigh(6)
+            for half in range(2):
+                nc.vector.tensor_tensor(out=y_of(7)[:, halves[half]], in0=odds[:, halves[half]], in1=sheet_sb[1][:, 3, halves[half]], op=ALU.mult)
+                nc.sync.dma_start(out=out_rows[1, 3][:, halves[half]], in_=y_of(7)[:, halves[half]])
 
         def planes(g, half, engine):
             m0, m1 = 256 * half, 256 * (half + 1)
-            grouped = interleave(engine, slots[g][:, :, M + m0:M + m1])
+            grouped = interleave(engine, y_rows[g][:, :, m0:m1])
             nc.vector.quantize_mx(out=y_codes[g][:, m0:m1].bitcast(FP8X4), scales=y_sc[g][:, m0:m1], in_=grouped[:])
             nc.sync.dma_start(out=out_1[g].rearrange("p m t -> p (m t)").bitcast(I32)[:, m0:m1],
                               in_=y_codes[g][:, m0:m1].bitcast(I32))
 
         def store_scales(g):
             for q in range(4):
-                nc.sync.dma_start(out=out_2[g, 4 * q:4 * q + 4, :].bitcast(I32), in_=y_sc[g][32 * q:32 * q + 4, :].bitcast(I32))
+                (nc.sync, nc.scalar)[g * (q // 2)].dma_start(out=out_2[g, 4 * q:4 * q + 4, :].bitcast(I32), in_=y_sc[g][32 * q:32 * q + 4, :].bitcast(I32))
 
-        score(0, 0)
-        score(0, 1)
+        for i in range(3):
+            score(i)
         for i in range(7):
-            second = pick_second(i, 0, M)
-            score(i + 1, 0)
-            score(i + 1, 1)
-            odds = compare(i, 0, M, second)
-            weigh(i, 0, M, odds)
-            if i == 1:
-                quantize_weight(w3_raw[1], w3_codes[1], w3_sc[1], ("scalar", "scalar"))
-            if i == 3:
+            if i in (0, 2):
+                quantize_weight_half(w3_raw[1], w3_codes[1], w3_sc[1], i // 2, "scalar")
+            if i + 3 < 8:
+                score(i + 3)
+            compare(i)
+            if i >= 1:
+                weigh(i - 1)
+            if i == 5:
                 planes(0, 0, "scalar")
                 planes(0, 1, "scalar")
                 store_scales(0)
-        seconds = [pick_second(7, 256 * half, 256 * (half + 1)) for half in range(2)]
-        odds_halves = [compare(7, 256 * half, 256 * (half + 1), seconds[half]) for half in range(2)]
-        for half in range(2):
-            weigh(7, 256 * half, 256 * (half + 1), odds_halves[half])
+        finish_last_tile()
         planes(1, 0, "scalar")
         planes(1, 1, "vector")
         store_scales(1)

@@ -41,9 +41,9 @@ def tile_list_rival_form_scores_kernel(tc, tab_words, tab_scales, offs, pos1, po
         w2_sc_raw = held.tile([P, 2 * H], U8, name="w2_sc_raw", align_bytes=64)
         nc.vector.memset(tab_sc[:].bitcast(I32), 0)
         nc.vector.memset(w2_sc_raw[:].bitcast(I32), 0)
-        for q in range(4):
-            nc.sync.dma_start(out=tab_sc[32 * q:32 * q + 4, :].bitcast(I32).rearrange("r (a t) -> r a t", a=2),
-                                in_=tab_scales[:, 4 * q:4 * q + 4, :].rearrange("a r t -> r a t").bitcast(I32))
+        for r in range(4):
+            nc.sync.dma_start(out=tab_sc[r:P:32, :].bitcast(I32).rearrange("q (a t) -> q a t", a=2),
+                              in_=tab_scales.rearrange("a (q r) t -> r q a t", r=4)[r].bitcast(I32))
 
         def four_rows():
             return ring.tile([P, 4, BANK], F32, name="four_rows", tag="four_rows", bufs=5)
@@ -85,11 +85,12 @@ def tile_list_rival_form_scores_kernel(tc, tab_words, tab_scales, offs, pos1, po
         sheet_rows = sheet.rearrange("(g p t) m -> g p t m", g=2, t=4)
         out_rows = out_0.rearrange("(g p t) m -> g t p m", g=2, t=4)
         sheet_sb = {}
-        pages = {}
+        two_pages = [held.tile([P, 2 * S], F32, name="page%d" % u) for u in range(2)]
+        pages = [two_pages[i % 2] for i in range(8)]
+        going_sb = [two_pages[i][:, S:] if i < 2 else held.tile([P, S], F32, name="going%d" % i)[:] for i in range(8)]
 
         def load_going(i):
-            pages[i] = ring.tile([P, 2 * S], F32, name="page", tag="page", bufs=8)
-            nc.sync.dma_start(out=pages[i][:, S:], in_=going_rows[i // 4, i % 4])
+            nc.sync.dma_start(out=going_sb[i], in_=going_rows[i // 4, i % 4])
 
         def load_sheet(g):
             sheet_sb[g] = four_rows()
@@ -136,8 +137,6 @@ def tile_list_rival_form_scores_kernel(tc, tab_words, tab_scales, offs, pos1, po
                                       in_=w2_sc_raw[:].rearrange("p (a m t) -> p a m t", a=2, t=4))
             for c in range(2):
                 nc.vector.tensor_copy(v_codes[a][c][:], tab_w[a][:].bitcast(U32).indirect(offs_sb[:, 32 * c:32 * (c + 1)]))
-        quantize_weight(w1_raw[0], w1_codes[0], w1_sc[0], ("scalar", "vector"))
-        quantize_weight(w1_raw[1], w1_codes[1], w1_sc[1], ("vector", "scalar"))
 
         squares = {}
         for c in range(2):
@@ -152,7 +151,10 @@ def tile_list_rival_form_scores_kernel(tc, tab_words, tab_scales, offs, pos1, po
                 square = ring.tile([P, BANK], F32, name="square", tag="square", bufs=8)
                 nc.scalar.activation(out=square[:], in_=b_bank[:], func=ACT.Square)
                 squares[c, t] = square
-        quantize_weight(w3_raw[0], w3_codes[0], w3_sc[0], ("scalar", "scalar"))
+            if c == 0:
+                quantize_weight(w1_raw[0], w1_codes[0], w1_sc[0], ("vector", "vector"))
+                quantize_weight(w1_raw[1], w1_codes[1], w1_sc[1], ("vector", "scalar"))
+        quantize_weight_half(w3_raw[0], w3_codes[0], w3_sc[0], 0, "scalar")
         h_codes = held.tile([P, S], U32, name="h_codes", align_bytes=64)
         h_sc = held.tile([P, S], U8, name="h_sc", align_bytes=64)
         h_rows = [held.tile([P, 4, BANK], BF16, name="h_rows%d" % c) for c in range(2)]
@@ -173,9 +175,10 @@ def tile_list_rival_form_scores_kernel(tc, tab_words, tab_scales, offs, pos1, po
                     rows.rearrange("p t (c i) -> p c t i", i=4))
             return grouped
 
-        h_grouped = [interleave(("scalar", "vector")[piece // 2], h_rows[piece // 2][:, :, 256 * (piece % 2):256 * (piece % 2 + 1)])
+        h_grouped = [interleave("vector" if piece == 2 else "scalar", h_rows[piece // 2][:, :, 256 * (piece % 2):256 * (piece % 2 + 1)])
                      for piece in range(4)]
-        for piece in range(4):
+
+        def quantize_h(piece):
             cols = slice(256 * piece, 256 * (piece + 1))
             nc.vector.quantize_mx(out=h_codes[:, cols].bitcast(FP8X4), scales=h_sc[:, cols], in_=h_grouped[piece][:])
 
@@ -186,22 +189,19 @@ def tile_list_rival_form_scores_kernel(tc, tab_words, tab_scales, offs, pos1, po
         first_pick = held.tile([P, M], F32, name="first_pick")
         odds_banks = {}
 
-        def score(i):
+        def score(i, c):
             g, t = divmod(i, 4)
-            page = pages[i]
-            for c in range(2):
-                cols = slice(BANK * c, BANK * (c + 1))
-                given = page[:, S + BANK * c:S + BANK * (c + 1)]
-                bank = psum.tile([P, BANK], F32, name="score_bank", tag="product", bufs=4)
-                nc.tensor.matmul_mx(out=bank[:], lhsT=w3_codes[g][:, P * t:P * (t + 1)].bitcast(FP8X4),
-                                    lhsT_scale=w3_sc[g][:, P * t:P * (t + 1)],
-                                    rhs=h_codes[:, cols].bitcast(FP8X4), rhs_scale=h_sc[:, cols], start=True, stop=True)
-                if i == 0:
-                    nc.vector.tensor_tensor(out=page[:, cols], in0=bank[:], in1=given, op=ALU.add)
-                else:
-                    nc.scalar.copy(out=page[:, cols], in_=bank[:])
-            if i > 0:
-                nc.gpsimd.tensor_tensor(out=page[:, :S], in0=page[:, :S], in1=page[:, S:], op=ALU.add)
+            cols = slice(BANK * c, BANK * (c + 1))
+            bank = psum.tile([P, BANK], F32, name="score_bank", tag="product", bufs=4)
+            nc.tensor.matmul_mx(out=bank[:], lhsT=w3_codes[g][:, P * t:P * (t + 1)].bitcast(FP8X4),
+                                lhsT_scale=w3_sc[g][:, P * t:P * (t + 1)],
+                                rhs=h_codes[:, cols].bitcast(FP8X4), rhs_scale=h_sc[:, cols], start=True, stop=True)
+            if c == 0 or i == 0:
+                nc.vector.tensor_tensor(out=pages[i][:, cols], in0=bank[:], in1=going_sb[i][:, cols], op=ALU.add)
+            else:
+                product = ring.tile([P, BANK], F32, name="product", tag="product", bufs=3)
+                nc.scalar.copy(out=product[:], in_=bank[:])
+                nc.gpsimd.tensor_tensor(out=pages[i][:, cols], in0=product[:], in1=going_sb[i][:, cols], op=ALU.add)
 
         def y_of(i):
             return y_rows[i // 4][:, i % 4, :]
@@ -256,14 +256,21 @@ def tile_list_rival_form_scores_kernel(tc, tab_words, tab_scales, offs, pos1, po
             for q in range(4):
                 (nc.sync, nc.scalar)[g * (q // 2)].dma_start(out=out_2[g, 4 * q:4 * q + 4, :].bitcast(I32), in_=y_sc[g][32 * q:32 * q + 4, :].bitcast(I32))
 
-        for i in range(3):
-            score(i)
+        for piece in range(3):
+            quantize_h(piece)
+        score(0, 0)
+        quantize_h(3)
+        score(1, 1)
+        score(0, 1)
+        score(1, 0)
+        quantize_weight_half(w3_raw[0], w3_codes[0], w3_sc[0], 1, "scalar")
         for i in range(7):
-            if i in (0, 2):
-                quantize_weight_half(w3_raw[1], w3_codes[1], w3_sc[1], i // 2, "scalar")
-            if i + 3 < 8:
-                score(i + 3)
             compare(i)
+            if i in (1, 2):
+                quantize_weight_half(w3_raw[1], w3_codes[1], w3_sc[1], i - 1, "scalar")
+            if i + 2 < 8:
+                score(i + 2, 1)
+                score(i + 2, 0)
             if i >= 1:
                 weigh(i - 1)
             if i == 5:

from contextlib import ExitStack

import concourse.mybir as mybir
from concourse.masks import make_identity

K, T, S, M, H, N = 1024, 4096, 1024, 512, 512, 1024
FLOPS = 2 * K * H * S * 2 + 2 * H * N * S

F32 = mybir.dt.float32
BF16 = mybir.dt.bfloat16
I32 = mybir.dt.int32
U32 = mybir.dt.uint32
U16 = mybir.dt.uint16
U8 = mybir.dt.uint8
FP8X4 = mybir.dt.float8_e4m3fn_x4
FP4X4 = mybir.dt.float4_e2m1fn_x4
ALU = mybir.AluOpType
ACT = mybir.ActivationFunctionType
P = 128
BANK = 512


def tile_list_rival_form_scores_kernel(tc, tab_words, tab_scales, offs, pos1, pos2, w1, w2_words, w2_scales,
                                                 gain, w3, going, sheet, out_0, out_1, out_2):
    nc = tc.nc
    with ExitStack() as ctx:
        held = ctx.enter_context(tc.tile_pool(name="held", bufs=1))
        ring = ctx.enter_context(tc.tile_pool(name="ring", bufs=2))
        psum = ctx.enter_context(tc.psum_pool(name="psum", bufs=2))

        def copy_on(engine, out, in_):
            if engine == "scalar":
                nc.scalar.copy(out=out, in_=in_)
            else:
                nc.vector.tensor_copy(out=out, in_=in_)

        def staged():
            return ring.tile([P, 1024], BF16, name="staged", tag="staged", bufs=8, align_bytes=64)

        tab_sc = held.tile([P, 2 * T], U8, name="tab_sc", align_bytes=64)
        w2_sc_raw = held.tile([P, 2 * H], U8, name="w2_sc_raw", align_bytes=64)
        nc.vector.memset(tab_sc[:].bitcast(I32), 0)
        nc.vector.memset(w2_sc_raw[:].bitcast(I32), 0)
        for r in range(4):
            nc.sync.dma_start(out=tab_sc[r:P:32, :].bitcast(I32).rearrange("q (a t) -> q a t", a=2),
                              in_=tab_scales.rearrange("a (q r) t -> r q a t", r=4)[r].bitcast(I32))

        def four_rows():
            return ring.tile([P, 4, BANK], F32, name="four_rows", tag="four_rows", bufs=5)

        tab_w = [held.tile([P, T], I32, name="tab_w%d" % a, align_bytes=64) for a in range(2)]
        tab_rows = [tab_words[a].rearrange("p t i -> p (t i)").bitcast(I32) for a in range(2)]

        def load_table_columns(a, first, last):
            nc.sync.dma_start(out=tab_w[a][:, first:last], in_=tab_rows[a][:, first:last])

        offs_sb = held.tile([P, S // 16], U16, name="offs_sb")
        nc.sync.dma_start(offs_sb[:], offs)
        pos1_sb = held.tile([P, M // 16], U16, name="pos1_sb")
        nc.sync.dma_start(pos1_sb[:], pos1)
        pos2_sb = held.tile([P, M // 16], U16, name="pos2_sb")
        nc.sync.dma_start(pos2_sb[:], pos2)
        gain_sb = held.tile([P, 4], F32, name="gain_sb")
        nc.sync.dma_start(out=gain_sb[:], in_=gain.rearrange("(p t) -> p t", t=4))
        w2_raw = held.tile([P, 4 * H], U8, name="w2_raw", align_bytes=64)
        for a in range(2):
            nc.sync.dma_start(out=w2_raw[:, 2 * H * a:2 * H * (a + 1)].bitcast(I32), in_=w2_words[a].bitcast(I32))
        load_table_columns(0, 0, 1536)
        load_table_columns(0, 1536, 3072)
        load_table_columns(0, 3072, T)
        load_table_columns(1, 0, 3072)
        for q in range(4):
            nc.sync.dma_start(out=w2_sc_raw[32 * q:32 * q + 4, :].bitcast(I32).rearrange("r (a c) -> r a c", a=2),
                                in_=w2_scales[:, 4 * q:4 * q + 4, :].rearrange("a r c -> r a c").bitcast(I32))
        load_table_columns(1, 3072, T)
        w1_raw = [four_rows() for a in range(2)]
        w1_rows = w1.rearrange("(a p i) r -> a p i r", a=2, i=4)
        for a in range(2):
            nc.sync.dma_start(out=w1_raw[a][:], in_=w1_rows[a])
        w3_raw = [four_rows() for g in range(2)]
        w3_rows = w3.rearrange("(p i) (g n) -> g p i n", i=4, g=2)
        nc.sync.dma_start(out=w3_raw[0][:], in_=w3_rows[0])

        going_rows = going.rearrange("(g p t) j -> g t p j", g=2, t=4)
        sheet_rows = sheet.rearrange("(g p t) m -> g p t m", g=2, t=4)
        out_rows = out_0.rearrange("(g p t) m -> g t p m", g=2, t=4)
        sheet_sb = {}
        two_pages = [held.tile([P, 2 * S], F32, name="page%d" % u) for u in range(2)]
        pages = [two_pages[i % 2] for i in range(8)]
        going_sb = [two_pages[i][:, S:] if i < 2 else held.tile([P, S], F32, name="going%d" % i)[:] for i in range(8)]

        def load_going(i):
            nc.sync.dma_start(out=going_sb[i], in_=going_rows[i // 4, i % 4])

        def load_sheet(g):
            sheet_sb[g] = four_rows()
            nc.sync.dma_start(out=sheet_sb[g][:], in_=sheet_rows[g])

        load_going(0)
        load_going(1)
        nc.sync.dma_start(out=w3_raw[1][:], in_=w3_rows[1])
        load_going(2)
        load_sheet(0)
        load_going(3)
        for i in range(4, 8):
            load_going(i)
        identity = held.tile([P, P], F32, name="identity")
        make_identity(nc, identity[:])

        w2_codes = held.tile([P, 4 * H], U8, name="w2_codes", align_bytes=64)
        w2_sc = held.tile([P, 2 * H], U8, name="w2_sc", align_bytes=64)
        nc.vector.tensor_copy(out=w2_codes[:].bitcast(U16).rearrange("p (a t m) -> p a m t", a=2, t=4),
                              in_=w2_raw[:].bitcast(U16).rearrange("p (a m t) -> p a m t", a=2, t=4))

        def quantize_weight_half(raw, codes, scales, u, engine):
            grouped = staged()
            copy_on(engine, grouped[:].rearrange("p (t m i) -> p m i t", t=2, i=4),
                    raw[:].rearrange("p i (m t) -> p m i t", t=4)[:, :, :, 2 * u:2 * u + 2])
            cols = slice(256 * u, 256 * (u + 1))
            nc.vector.quantize_mx(out=codes[:, cols].bitcast(FP8X4), scales=scales[:, cols], in_=grouped[:])

        def quantize_weight(raw, codes, scales, engines):
            for u in range(2):
                quantize_weight_half(raw, codes, scales, u, engines[u])

        w1_codes = [held.tile([P, H], U32, name="w1_codes%d" % a, align_bytes=64) for a in range(2)]
        w1_sc = [held.tile([P, H], U8, name="w1_sc%d" % a, align_bytes=64) for a in range(2)]
        w3_codes = [held.tile([P, BANK], U32, name="w3_codes%d" % g, align_bytes=64) for g in range(2)]
        w3_sc = [held.tile([P, BANK], U8, name="w3_sc%d" % g, align_bytes=64) for g in range(2)]

        v_codes = [[held.tile([P, BANK], U32, name="v_codes%d%d" % (a, c), align_bytes=64) for c in range(2)] for a in range(2)]
        v_sc = [held.tile([P, S], U8, name="v_sc%d" % a, align_bytes=64) for a in range(2)]
        for a in range(2):
            nc.vector.tensor_copy(v_sc[a][:], tab_sc[:, a * T:(a + 1) * T].indirect(offs_sb[:]))
            if a == 0:
                nc.vector.tensor_copy(out=w2_sc[:].rearrange("p (a t m) -> p a m t", a=2, t=4),
                                      in_=w2_sc_raw[:].rearrange("p (a m t) -> p a m t", a=2, t=4))
            for c in range(2):
                nc.vector.tensor_copy(v_codes[a][c][:], tab_w[a][:].bitcast(U32).indirect(offs_sb[:, 32 * c:32 * (c + 1)]))

        squares = {}
        for c in range(2):
            for t in range(4):
                b_bank = psum.tile([P, BANK], F32, name="b_bank", tag="product", bufs=4)
                for a in range(2):
                    col = 4 * a + t
                    nc.tensor.matmul_mx(out=b_bank[:], lhsT=w2_codes[:, 256 * col:256 * (col + 1)].bitcast(FP4X4),
                                        lhsT_scale=w2_sc[:, P * col:P * (col + 1)],
                                        rhs=v_codes[a][c][:].bitcast(FP8X4), rhs_scale=v_sc[a][:, BANK * c:BANK * (c + 1)],
                                        start=(a == 0), stop=(a == 1))
                square = ring.tile([P, BANK], F32, name="square", tag="square", bufs=8)
                nc.scalar.activation(out=square[:], in_=b_bank[:], func=ACT.Square)
                squares[c, t] = square
            if c == 0:
                quantize_weight(w1_raw[0], w1_codes[0], w1_sc[0], ("vector", "vector"))
                quantize_weight(w1_raw[1], w1_codes[1], w1_sc[1], ("vector", "scalar"))
        quantize_weight_half(w3_raw[0], w3_codes[0], w3_sc[0], 0, "scalar")
        h_codes = held.tile([P, S], U32, name="h_codes", align_bytes=64)
        h_sc = held.tile([P, S], U8, name="h_sc", align_bytes=64)
        h_rows = [held.tile([P, 4, BANK], BF16, name="h_rows%d" % c) for c in range(2)]
        for c in range(2):
            for t in range(4):
                a_bank = psum.tile([P, BANK], F32, name="a_bank", tag=("diff", "odds")[t % 2])
                for a in range(2):
                    nc.tensor.matmul_mx(out=a_bank[:], lhsT=w1_codes[a][:, P * t:P * (t + 1)].bitcast(FP8X4),
                                        lhsT_scale=w1_sc[a][:, P * t:P * (t + 1)],
                                        rhs=v_codes[a][c][:].bitcast(FP8X4), rhs_scale=v_sc[a][:, BANK * c:BANK * (c + 1)],
                                        start=(a == 0), stop=(a == 1))
                nc.vector.scalar_tensor_tensor(out=h_rows[c][:, t, :], in0=a_bank[:], scalar=gain_sb[:, t:t + 1],
                                               in1=squares[c, t][:], op0=ALU.mult, op1=ALU.mult)

        def interleave(engine, rows):
            grouped = staged()
            copy_on(engine, grouped[:].rearrange("p (c i t) -> p c t i", i=4, t=4),
                    rows.rearrange("p t (c i) -> p c t i", i=4))
            return grouped

        h_grouped = [interleave("vector" if piece == 2 else "scalar", h_rows[piece // 2][:, :, 256 * (piece % 2):256 * (piece % 2 + 1)])
                     for piece in range(4)]

        def quantize_h(piece):
            cols = slice(256 * piece, 256 * (piece + 1))
            nc.vector.quantize_mx(out=h_codes[:, cols].bitcast(FP8X4), scales=h_sc[:, cols], in_=h_grouped[piece][:])

        y_codes = [held.tile([P, M], U32, name="y_codes%d" % g, align_bytes=64) for g in range(2)]
        y_sc = [held.tile([P, M], U8, name="y_sc%d" % g, align_bytes=64) for g in range(2)]
        load_sheet(1)
        y_rows = [four_rows() for g in range(2)]
        first_pick = held.tile([P, M], F32, name="first_pick")
        odds_banks = {}

        def score(i, c):
            g, t = divmod(i, 4)
            cols = slice(BANK * c, BANK * (c + 1))
            bank = psum.tile([P, BANK], F32, name="score_bank", tag="product", bufs=4)
            nc.tensor.matmul_mx(out=bank[:], lhsT=w3_codes[g][:, P * t:P * (t + 1)].bitcast(FP8X4),
                                lhsT_scale=w3_sc[g][:, P * t:P * (t + 1)],
                                rhs=h_codes[:, cols].bitcast(FP8X4), rhs_scale=h_sc[:, cols], start=True, stop=True)
            if c == 0 or i == 0:
                nc.vector.tensor_tensor(out=pages[i][:, cols], in0=bank[:], in1=going_sb[i][:, cols], op=ALU.add)
            else:
                product = ring.tile([P, BANK], F32, name="product", tag="product", bufs=3)
                nc.scalar.copy(out=product[:], in_=bank[:])
                nc.gpsimd.tensor_tensor(out=pages[i][:, cols], in0=product[:], in1=going_sb[i][:, cols], op=ALU.add)

        def y_of(i):
            return y_rows[i // 4][:, i % 4, :]

        def compare(i):
            plus = first_pick[:] if i == 0 else y_of(i - 1)
            nc.vector.tensor_copy(plus, pages[i][:].indirect(pos1_sb[:]))
            minus = ring.tile([P, M], F32, name="minus", tag="minus", bufs=2)
            nc.vector.tensor_scalar(minus[:], pages[i][:].indirect(pos2_sb[:]), -1.0, 0.0, ALU.mult, ALU.add)
            diff_bank = psum.tile([P, BANK], F32, name="diff_bank", tag="diff")
            for term, picked in enumerate((plus, minus[:])):
                for b in range(4):
                    nc.tensor.matmul(diff_bank[:, P * b:P * (b + 1)], lhsT=picked[:, P * b:P * (b + 1)], rhs=identity[:],
                                     is_transpose=True, start=(term == 0 and b == 0), stop=(term == 1 and b == 3))
            odds_turned = ring.tile([P, M], F32, name="odds_turned", tag="odds_turned", bufs=2)
            nc.scalar.activation(out=odds_turned[:], in_=diff_bank[:], func=ACT.Sigmoid)
            odds_banks[i] = psum.tile([P, BANK], F32, name="odds_bank", tag="odds")
            for b in range(4):
                nc.tensor.transpose(odds_banks[i][:, P * b:P * (b + 1)], odds_turned[:, P * b:P * (b + 1)], identity[:])

        def weigh(i):
            g, t = divmod(i, 4)
            nc.vector.tensor_tensor(out=y_of(i), in0=odds_banks[i][:], in1=sheet_sb[g][:, t, :], op=ALU.mult)
            nc.sync.dma_start(out=out_rows[g, t], in_=y_of(i))

        def finish_last_tile():
            page = pages[7]
            halves = [slice(256 * half, 256 * (half + 1)) for half in range(2)]
            entries = [slice(16 * half, 16 * (half + 1)) for half in range(2)]
            minus = [y_of(6)[:, halves[0]], first_pick[:, halves[1]]]
            diff = ring.tile([P, M], F32, name="minus", tag="minus", bufs=2)
            odds = ring.tile([P, M], F32, name="odds_turned", tag="odds_turned", bufs=2)
            for half in range(2):
                nc.vector.tensor_copy(minus[half], page[:].indirect(pos2_sb[:, entries[half]]))
            for half in range(2):
                nc.vector.tensor_tensor(diff[:, halves[half]], page[:].indirect(pos1_sb[:, entries[half]]), minus[half], ALU.subtract)
                nc.scalar.activation(out=odds[:, halves[half]], in_=diff[:, halves[half]], func=ACT.Sigmoid)
                if half == 0:
                    weigh(6)
            for half in range(2):
                nc.vector.tensor_tensor(out=y_of(7)[:, halves[half]], in0=odds[:, halves[half]], in1=sheet_sb[1][:, 3, halves[half]], op=ALU.mult)
                nc.sync.dma_start(out=out_rows[1, 3][:, halves[half]], in_=y_of(7)[:, halves[half]])

        def planes(g, half, engine):
            m0, m1 = 256 * half, 256 * (half + 1)
            grouped = interleave(engine, y_rows[g][:, :, m0:m1])
            nc.vector.quantize_mx(out=y_codes[g][:, m0:m1].bitcast(FP8X4), scales=y_sc[g][:, m0:m1], in_=grouped[:])
            nc.sync.dma_start(out=out_1[g].rearrange("p m t -> p (m t)").bitcast(I32)[:, m0:m1],
                              in_=y_codes[g][:, m0:m1].bitcast(I32))

        def store_scales(g):
            for q in range(4):
                (nc.sync, nc.scalar)[g * (q // 2)].dma_start(out=out_2[g, 4 * q:4 * q + 4, :].bitcast(I32), in_=y_sc[g][32 * q:32 * q + 4, :].bitcast(I32))

        for piece in range(3):
            quantize_h(piece)
        score(0, 0)
        quantize_h(3)
        score(1, 1)
        score(0, 1)
        score(1, 0)
        quantize_weight_half(w3_raw[0], w3_codes[0], w3_sc[0], 1, "scalar")
        for i in range(7):
            compare(i)
            if i in (1, 2):
                quantize_weight_half(w3_raw[1], w3_codes[1], w3_sc[1], i - 1, "scalar")
            if i + 2 < 8:
                score(i + 2, 1)
                score(i + 2, 0)
            if i >= 1:
                weigh(i - 1)
            if i == 5:
                planes(0, 0, "scalar")
                planes(0, 1, "scalar")
                store_scales(0)
        finish_last_tile()
        planes(1, 0, "scalar")
        planes(1, 1, "vector")
        store_scales(1)
